import numpy as np
import ml_dtypes


def mxq(x, axis, fmt="e4m3"):
    dtype, down = {"e4m3": (ml_dtypes.float8_e4m3fn, 7), "e5m2": (ml_dtypes.float8_e5m2, 14)}[fmt]
    v = np.moveaxis(np.asarray(x, np.float32).astype(ml_dtypes.bfloat16).astype(np.float64), axis, -1)
    blocks = v.reshape(v.shape[:-1] + (-1, 32))
    amax = np.abs(blocks).max(-1, keepdims=True)
    byte = np.maximum(np.where(amax > 0, np.frexp(amax)[1] - 1 + 127, 0) - down, 1)
    scale = np.exp2(byte - 127.0)
    codes = (blocks / scale).astype(np.float32).astype(dtype).astype(np.float64)
    return np.moveaxis((codes * scale).reshape(v.shape), -1, axis)


WIDE = False


def mx_kscale(k):
    if not WIDE:
        return np.ones(k)
    levels = np.array([10, -10, 5, -5, 0])
    if k % 512:
        return np.exp2(np.random.permutation(np.resize(levels, k // 32))).repeat(32)
    a = np.empty((k // 512, 16))
    for p in range(k // 512):
        a[p, :8] = np.random.permutation(np.resize(levels, 8))
        for g in range(8):
            far = levels[np.abs(levels - a[p, g]) >= 10]
            a[p, g + 8] = far[np.random.randint(len(far))]
    return np.exp2(a.ravel()).repeat(32)


def f64(x):
    return np.asarray(x).astype(np.float64)


def striped(idx):
    return np.tile(np.asarray(idx).reshape(-1, 16).T, (8, 1)).astype(np.uint16)


def unstriped(offs):
    return offs[:16].T.reshape(-1).astype(np.int64)


def striped8(idx):
    return np.asarray(idx).reshape(8, -1, 16).transpose(0, 2, 1).reshape(128, -1).astype(np.uint16)


def unstriped8(offs):
    return offs.reshape(8, 16, -1).transpose(0, 2, 1).reshape(8, -1).astype(np.int64)


def pick8(x, idx, run):
    r = np.arange(len(x))
    return x[r[:, None], idx[r % (8 * run) // run]]


E2M1 = np.array([0.0, 0.5, 1.0, 1.5, 2.0, 3.0, 4.0, 6.0, -0.0, -0.5, -1.0, -1.5, -2.0, -3.0, -4.0, -6.0])


def pack_weight(w, fmt):
    k, n = w.shape
    w = f64(np.asarray(w, np.float32).astype(ml_dtypes.bfloat16)).reshape(k // 32, 32, n)
    amax = np.abs(w).max(1)
    if fmt == "e4m3":
        byte = np.frexp(amax)[1] - 1 + 127 - 7
    else:
        mant, ex = np.frexp(amax / 6.0)
        byte = np.where(mant > 0.5, ex, ex - 1) + 127
    byte = np.clip(np.where(amax > 0, byte, 1), 1, 254)
    scaled = (w * np.exp2(127.0 - byte)[:, None, :]).reshape(k, n).astype(np.float32)
    by_word = np.ascontiguousarray(scaled.reshape(k // 512, 128, 4, n).transpose(0, 1, 3, 2))
    if fmt == "e4m3":
        words = by_word.astype(ml_dtypes.float8_e4m3fn).view(np.uint8)
    else:
        c = by_word.astype(ml_dtypes.float4_e2m1fn).view(np.uint8) & 0xF
        words = (c[..., 0::2] | (c[..., 1::2] << 4)).reshape(k // 512, 128, 2 * n)
    return np.ascontiguousarray(words), np.ascontiguousarray(byte.astype(np.uint8).reshape(k // 512, 16, n))


def unpack_weight(words, scales, fmt):
    g, _, n = scales.shape
    words = np.ascontiguousarray(words).reshape(g, 128, n, -1)
    if fmt == "e4m3":
        vals = words.view(ml_dtypes.float8_e4m3fn).astype(np.float64)
    else:
        nib = np.empty((g, 128, n, 4), np.uint8)
        nib[..., 0::2] = words & 0xF
        nib[..., 1::2] = words >> 4
        vals = E2M1[nib]
    vals = vals * np.repeat(np.exp2(scales.astype(np.float64) - 127.0), 8, axis=1)[..., None]
    return vals.transpose(0, 1, 3, 2).reshape(g * 512, n)


def sigmoid(v):
    return 1.0 / (1.0 + np.exp(-v))


def sgn(shape):
    return np.random.uniform(0.5, 2.0, shape) * np.where(np.random.standard_normal(shape) < 0, -1.0, 1.0)


K, J, R, T, Z, M, O, C, N, S = 512, 512, 512, 2048, 512, 1024, 192, 256, 256, 1024


def setup_inputs():
    n = np.random.standard_normal
    idx = np.random.permutation(T)[:J]
    idx2 = np.random.permutation(M)[:J]
    idx3 = np.stack([np.random.permutation(J)[:O] for _ in range(8)])
    idx4 = np.stack([np.random.permutation(C)[:O] for _ in range(8)])
    idx5 = np.stack([np.random.permutation(J)[:C] for _ in range(8)])
    idx6 = np.random.permutation(S)[:N]
    fk = mx_kscale(K)
    fr = mx_kscale(R)
    fz = mx_kscale(Z)
    xtp = pack_weight(n((K, T)) * fk[:, None], "e4m3")
    wp = pack_weight(n((K, R)) * 1 / np.sqrt(K) / fk[:, None] * fr, "e2m1")
    xop = pack_weight(n((Z, M)) / fz[:, None], "e2m1")
    w2p = pack_weight(n((Z, R)) * 1 / np.sqrt(Z) * fz[:, None], "e4m3")
    vsp = pack_weight(n((R, S)) * 1 / np.sqrt(R) / fr[:, None], "e4m3")
    return {
        "xt_words": xtp[0],
        "xt_scales": xtp[1],
        "w_words": wp[0],
        "w_scales": wp[1],
        "xo_words": xop[0],
        "xo_scales": xop[1],
        "w2_words": w2p[0],
        "w2_scales": w2p[1],
        "sl": (sgn((R, 1))).astype(np.float32),
        "gf": (np.random.uniform(-1.0, 1.0, (R, 1))).astype(np.float32),
        "sa": (np.random.uniform(0.5, 1.6, (R, 1))).astype(np.float32),
        "vs_words": vsp[0],
        "vs_scales": vsp[1],
        "offs": striped(idx),
        "offs2": striped(idx2),
        "offs3": striped8(idx3),
        "offs4": striped8(idx4),
        "offs5": striped8(idx5),
        "offs6": striped(idx6),
    }


def reference(xt_words, xt_scales, w_words, w_scales, xo_words, xo_scales, w2_words, w2_scales, sl, gf, sa, vs_words, vs_scales, offs, offs2, offs3, offs4, offs5, offs6):
    idx = unstriped(offs)
    idx2 = unstriped(offs2)
    idx3 = unstriped8(offs3)
    idx4 = unstriped8(offs4)
    idx5 = unstriped8(offs5)
    idx6 = unstriped(offs6)
    xtu = unpack_weight(xt_words, xt_scales, "e4m3")
    wu = unpack_weight(w_words, w_scales, "e2m1")
    xou = unpack_weight(xo_words, xo_scales, "e2m1")
    w2u = unpack_weight(w2_words, w2_scales, "e4m3")
    vsu = unpack_weight(vs_words, vs_scales, "e4m3")
    xtidxg = xtu[:, idx]
    a = wu.T @ xtidxg
    xoidx2g = xou[:, idx2]
    b = w2u.T @ xoidx2g
    h1 = pick8(a, idx3, 64) * f64(sa)
    pw = np.zeros((R, C))
    pw[np.arange(R)[:, None], idx4[np.arange(R) % 512 // 64]] = h1
    hid = pw * sigmoid(pick8(b, idx5, 64) * f64(sl) + f64(gf))
    vsidx6g = vsu[:, idx6]
    hidq = mxq(hid, 0, "e4m3")
    y = vsidx6g.T @ hidq
    return y

from contextlib import ExitStack

import concourse.mybir as mybir

F32 = mybir.dt.float32
BF16 = mybir.dt.bfloat16
I32 = mybir.dt.int32
U32 = mybir.dt.uint32
U16 = mybir.dt.uint16
U8 = mybir.dt.uint8
FP8X4 = mybir.dt.float8_e4m3fn_x4
FP4X4 = mybir.dt.float4_e2m1fn_x4
ACT = mybir.ActivationFunctionType
MULT = mybir.AluOpType.mult

K, J, R, T, Z, M, O, C, N, S = 512, 512, 512, 2048, 512, 1024, 192, 256, 256, 1024
P = 128
PACK = 4
ALIGN = 64

FLOPS = 2 * K * R * J + 2 * Z * R * J + 2 * R * N * C


def tile_picked_tokens_gate_two_gatedfill_store_plain_kernel(
    tc, xt_words, xt_scales, w_words, w_scales, xo_words, xo_scales, w2_words, w2_scales,
    sl, gf, sa, vs_words, vs_scales, offs, offs2, offs3, offs4, offs5, offs6, out,
):
    nc = tc.nc
    with ExitStack() as ctx:
        sb = ctx.enter_context(tc.tile_pool(name="sb", bufs=1))
        ps = ctx.enter_context(tc.psum_pool(name="ps", bufs=1))

        def tile(name, cols, dtype, tag=None):
            return sb.tile([P, cols], dtype, name=name, tag=tag or name, align_bytes=ALIGN)

        def load_list(name, src):
            lst = tile(name, src.shape[1], U16)
            nc.sync.dma_start(lst[:], src)
            return lst

        def load_words(name, src, cols, dtype, queue, tag=None):
            words = tile(name, cols, dtype, tag)
            queue.dma_start(words[:].bitcast(I32), src.bitcast(I32))
            return words

        def cleared_plane(name, cols, tag=None):
            plane = tile(name, cols, U8, tag)
            nc.vector.memset(plane[:].bitcast(I32), 0)
            return plane

        def load_scale_rows(plane, src, queue):
            rows = src[0].bitcast(I32)
            for i in range(4):
                queue.dma_start(plane[:].bitcast(I32)[i:P:32, :], rows[i:16:4, :])

        def load_column(name, src):
            col = tile(name, PACK, F32)
            nc.sync.dma_start(col[:], src.rearrange("(p t) o -> p (t o)", t=PACK))
            return col

        def e4m3_rows(src):
            return src[0].rearrange("p n t -> p (n t)")

        def load_staged_rows(name, src, cols):
            staged = sb.tile([4, 4, cols // 4], I32, name=name, align_bytes=ALIGN)
            nc.sync.dma_start(staged[:], src[0].bitcast(I32).rearrange("(q i) w -> i q w", i=4))
            return staged

        def spread(plane, staged):
            for q in range(4):
                nc.vector.tensor_copy(plane[:].bitcast(I32)[32 * q : 32 * q + 4, :], staged[:, q, :])

        xt_plane = cleared_plane("xt_plane", T)
        w_plane = cleared_plane("w_plane", R)
        pages = []
        for t in range(PACK):
            page = tile("page%d" % t, C, F32)
            nc.vector.memset(page[:], 0.0)
            pages.append(page)
        xo_plane = cleared_plane("xo_plane", M)
        vs_plane = cleared_plane("vs_plane", S)
        w2_plane = cleared_plane("w2_plane", R)

        w_staged = load_staged_rows("w_staged", w_scales, R)
        token_list = load_list("token_list", offs)
        w_raw = load_words("w_raw", w_words[0], R, U16, nc.sync)
        load_scale_rows(xt_plane, xt_scales, nc.sync)
        xt_table = load_words("xt_table", e4m3_rows(xt_words), T, U32, nc.sync)
        weight = load_column("weight", sa)
        notes_list = load_list("notes_list", offs2)
        xo_table = load_words("xo_table", xo_words[0], M, U16, nc.sync)
        put_list = load_list("put_list", offs4)
        w2_raw = load_words("w2_raw", e4m3_rows(w2_words), R, U32, nc.sync)
        take_list = load_list("take_list", offs3)
        store_list = load_list("store_list", offs6)
        load_scale_rows(xo_plane, xo_scales, nc.sync)
        vs_table = load_words("vs_table", e4m3_rows(vs_words), S, U32, nc.sync)
        gate_list = load_list("gate_list", offs5)
        slope = load_column("slope", sl)
        shift = load_column("shift", gf)
        load_scale_rows(w2_plane, w2_scales, nc.sync)
        load_scale_rows(vs_plane, vs_scales, nc.sync)

        def deal(copy, name, src, dtype, tag=None):
            dealt = tile(name, R, dtype, tag)
            copy(dealt[:].rearrange("p (t m) -> p m t", t=PACK), src[:].rearrange("p (m t) -> p m t", t=PACK))
            return dealt

        def deal_read(copy, name, src, dtype, tag=None):
            dealt = tile(name, R, dtype, tag)
            copy(dealt[:].rearrange("p (t m) -> p t m", t=PACK), src[:].rearrange("p (m t) -> p t m", t=PACK))
            return dealt

        def gather(name, table, lst, cols, dtype, pieces=None, tag=None):
            picked = tile(name, cols, dtype, tag)
            for piece in pieces or [slice(0, cols)]:
                nc.vector.tensor_copy(picked[:, piece], table[:].indirect(lst[:, piece.start // 16 : piece.stop // 16]))
            return picked

        pieces = [slice(0, J // 2), slice(J // 2, 3 * J // 4), slice(3 * J // 4, J)]

        w_dealt = deal_read(nc.scalar.copy, "w_dealt", w_raw, U16)
        spread(w_plane, w_staged)
        w_sc = deal_read(nc.vector.tensor_copy, "w_sc", w_plane, U8)
        xt_sc = gather("xt_sc", xt_plane, token_list, J, U8)
        xt_codes = gather("xt_codes", xt_table, token_list, J, U32, pieces)

        def product(bank, t, slots, lhs, lhs_sc, lhs_fmt, rhs, rhs_sc, rhs_fmt):
            acc = ps.tile([P, slots.stop - slots.start], F32, name="acc", tag="bank%d" % bank)
            cols = slice(t * P, (t + 1) * P)
            nc.tensor.matmul_mx(
                out=acc[:], lhsT=lhs[:, cols].bitcast(lhs_fmt), lhsT_scale=lhs_sc[:, cols],
                rhs=rhs[:, slots].bitcast(rhs_fmt), rhs_scale=rhs_sc[:, slots], start=True, stop=True,
            )
            return acc

        whole = slice(0, J)
        def rows_of(parts, name, tag=None):
            rows = tile(name, J, F32, tag)
            for copy, acc, slots in parts:
                copy(rows[:, slots], acc[:])
            return rows

        def take(t, rows):
            taken = tile("taken%d" % t, O, F32)
            nc.scalar.activation(
                out=taken[:], in_=rows[:].indirect(take_list[:]), func=ACT.Copy, scale=weight[:, t : t + 1]
            )
            return taken

        def put(t, taken):
            nc.scalar.activation(out=pages[t][:].indirect(put_list[:]), in_=taken[:], func=ACT.Copy)

        on_v, on_s = nc.vector.tensor_copy, nc.scalar.copy
        a_ops = (w_dealt, w_sc, FP4X4, xt_codes, xt_sc, FP8X4)
        rest = slice(pieces[1].start, J)
        jobs = [(0, pieces[0]), (1, pieces[0]), (0, pieces[1]), (0, pieces[2]), (1, rest), (2, whole), (3, whole)]
        a_parts = [[] for t in range(PACK)]
        for bank, (t, slots) in enumerate(jobs):
            a_parts[t].append((on_v if t else on_s, product(bank, t, slots, *a_ops), slots))
        taken = [take(0, rows_of(a_parts[0], "a_rows0"))]
        for t in range(1, PACK):
            taken.append(take(t, rows_of(a_parts[t], "a_rows%d" % t)))
            put(t - 1, taken[t - 1])
        put(PACK - 1, taken[PACK - 1])

        xo_codes = gather("xo_codes", xo_table, notes_list, J, U16)
        w2_dealt = deal(nc.vector.tensor_copy, "w2_dealt", w2_raw, U32)
        xo_sc = gather("xo_sc", xo_plane, notes_list, J, U8)
        w2_sc = deal_read(nc.vector.tensor_copy, "w2_sc", w2_plane, U8)
        b_ops = (w2_dealt, w2_sc, FP8X4, xo_codes, xo_sc, FP4X4)
        b_acc = [product((7 + t) % 8, t, whole, *b_ops) for t in range(PACK)]
        b_rows = [rows_of([(on_v, b_acc[t], whole)], "b_rows%d" % t) for t in range(PACK)]
        vs_codes = gather("vs_codes", vs_table, store_list, N, U32, tag="xo_codes")
        vs_sc = gather("vs_sc", vs_plane, store_list, N, U8)

        H = C // 2
        copies = (nc.scalar.copy, nc.vector.tensor_copy)
        queues = (nc.scalar, nc.sync)
        out_rows = out.rearrange("(g p) c -> p g c", p=P)
        quantised = []
        for h in range(2):
            cols = slice(h * H, (h + 1) * H)
            planes = sb.tile([P, PACK, H], BF16, name="planes%d" % h, align_bytes=ALIGN)
            for t in range(PACK):
                gate = tile("gate%d" % t, H, F32)
                nc.scalar.activation(
                    out=gate[:], in_=b_rows[t][:].indirect(gate_list[:, cols.start // 16 : cols.stop // 16]),
                    func=ACT.Sigmoid, scale=slope[:, t : t + 1], bias=shift[:, t : t + 1],
                )
                nc.vector.tensor_tensor(planes[:, t, :], pages[t][:, cols], gate[:], MULT)
            hid = tile("hid%d" % h, PACK * H, BF16)
            nc.vector.tensor_copy(hid[:].rearrange("p (c t) -> p c t", t=PACK), planes[:].rearrange("p t c -> p c t"))
            hid_codes = tile("hid_codes%d" % h, H, U32)
            hid_sc = tile("hid_sc%d" % h, H, U8)
            nc.vector.quantize_mx(out=hid_codes[:].bitcast(FP8X4), scales=hid_sc[:], in_=hid[:])
            quantised.append((hid_codes, hid_sc))

        def product_out(acc, g, h):
            feats = slice(g * P, (g + 1) * P)
            hid_codes, hid_sc = quantised[h]
            nc.tensor.matmul_mx(
                out=acc, lhsT=vs_codes[:, feats].bitcast(FP8X4), lhsT_scale=vs_sc[:, feats],
                rhs=hid_codes[:].bitcast(FP8X4), rhs_scale=hid_sc[:], start=True, stop=True,
            )

        acc = ps.tile([P, N // P, H], F32, name="y_left", tag="bank3")
        for g in range(N // P):
            product_out(acc[:, g, :], g, 0)
        left = sb.tile([P, N // P, H], F32, name="left", tag="b_rows%d" % (PACK - 1), align_bytes=ALIGN)
        nc.scalar.copy(left[:], acc[:])
        nc.scalar.dma_start(out_rows[:, :, :H], left[:])
        for g in range(N // P):
            acc = ps.tile([P, H], F32, name="y_right", tag="bank%d" % (4 + g))
            product_out(acc[:], g, 1)
            right = tile("right%d" % g, H, F32)
            copies[g](right[:], acc[:])
            queues[g].dma_start(out_rows[:, g, H:], right[:])
